import numpy as np, ml_dtypes
CORES = [19,27,51,107,147,155,179,235,275,283,307,363,403,411,435,491]
N = 16
import mx_ref
KO = 2
F = np.float32(0.7)
OWN = [5,6,9,11,5,5,6,6,9,9,11,11,5,6,9,11]
BF = ml_dtypes.bfloat16
def tile(rs):
    return np.stack(rs, axis=2).reshape(128, -1).astype(BF)
def pick(b):
    s = np.zeros((128, 128, 4), np.float32)
    s[np.arange(128), np.arange(128), b] = 1.0
    return mx_ref.quantize(s.reshape(128, 512).astype(BF))
def pk(c, s, i=0):
    return (np.ascontiguousarray(c[:, 512 * i:512 * i + 512]), mx_ref.live(s[:, 128 * i:128 * i + 128]))
def inputs(rng, e, E):
    def f(*shape):
        v = (rng.standard_normal(shape, dtype=np.float32) * np.exp2(rng.integers(-2, 3, shape[:-1] + (1,)))).astype(BF)
        return mx_ref.spread((v.astype(np.float32) * np.exp2(rng.integers(-E, E + 1, shape[:-2] + (1, 1))).astype(np.float32)).astype(BF), rng, e)
    def packed(k):
        c = np.zeros((N, 128, k * 512), np.uint8); s = np.zeros((N, 128, k * 128), np.uint8)
        for r in range(N):
            for i in range(k):
                a, b = mx_ref.quantize(f(128, 512)); c[r][:, 512 * i:512 * i + 512] = a; s[r][:, 128 * i:128 * i + 128] = mx_ref.plane(b, rng)
        return c, s
    d = {}
    d["kc"], d["ks"] = packed(KO)
    d["q"] = f(N, 128, 512)
    return d
def setup_inputs(rng):
    return inputs(rng, 0, 0)
def setup_inputs_blocks(rng):
    return inputs(rng, 4, 0)
def setup_inputs_wide(rng):
    return inputs(rng, 0, 8)
def reference(kc, ks, q):
    S = [pick(t) for t in range(4)]
    anew = lambda p, i: mx_ref.quantize(tile([mx_ref.matmul(S[t], pk(kc[p], ks[p], i)) * F for t in range(4)]))
    y = np.full((N, 128, 1024), np.nan, np.float32)
    for o in range(N):
        if OWN[o] != o: continue
        qq = mx_ref.quantize(q[o])
        M = [pk(kc[o], ks[o], i) for i in range(KO)] + [anew(p, i) for p in range(N) if p != o and OWN[p] == o for i in range(KO)]
        y[o][:, :128 * len(M)] = np.concatenate([mx_ref.matmul(qq, m) for m in M], axis=1)
    return {"y": y}

@@ -1,0 +1,191 @@
+import numpy as np
+from concourse.mybir import dt, AluOpType, ActivationFunctionType
+
+CORES_ALL = 512
+W = 128
+F = float(np.float32(0.7))
+PIECES = ("c0", "c1", "s")
+
+SCRATCH = {
+    "idx": ("sbuf", [128, 128], "float32"),
+    "e": ("sbuf", [128, 516], "bfloat16"),
+    "sc": ("sbuf", [128, 512], "float8_e4m3fn_x4"),
+    "ss": ("sbuf", [128, 512], "uint8"),
+    "kcb": ("sbuf", [128, 256], "float8_e4m3fn_x4"),
+    "ksb": ("sbuf", [128, 256], "uint8"),
+    "kt": ("sbuf", [128, 1024], "bfloat16"),
+    "nc": ("sbuf", [128, 256], "float8_e4m3fn_x4"),
+    "ns": ("sbuf", [128, 256], "uint8"),
+    "qt": ("sbuf", [128, 512], "bfloat16"),
+    "qc": ("sbuf", [128, 128], "float8_e4m3fn_x4"),
+    "qs": ("sbuf", [128, 128], "uint8"),
+    "mc": ("sbuf", [128, 1024], "float8_e4m3fn_x4"),
+    "ms": ("sbuf", [128, 1024], "uint8"),
+    "yt": ("sbuf", [128, 1024], "float32"),
+    "ps": ("psum", [128, 4096], "float32"),
+}
+SEMAPHORES = (["iota", "zero", "diag", "left", "relay", "lq", "lms", "lmc", "qq", "stored", "lks"]
+              + ["lk%d" % t for t in range(2)] + ["sq%d" % b for b in range(4)] + ["mm%d" % i for i in range(8)]
+              + ["made%d" % t for t in range(2)] + ["packed%d" % t for t in range(2)]
+              + ["a%d%s" % (k, p) for k in range(3) for p in PIECES] + ["cp%d" % k for k in range(4)])
+
+_plan = {}
+
+
+def relays(src, dst, cable_first, topo):
+    out = []
+    for c in range(CORES_ALL):
+        if topo.die(c) == topo.die(src) or not (topo.may_write(src, c) and topo.may_write(c, dst)):
+            continue
+        across = topo.rack(topo.host(c)) != topo.rack(topo.host(src))
+        if topo.host(c) in (topo.host(src), topo.host(dst)) or across != cable_first:
+            continue
+        if cable_first:
+            ok = topo.chip(c) == topo.chip(src)
+        else:
+            ok = topo.same_plane(src, c) and (topo.chip(c) == topo.chip(dst) or any(
+                topo.mates(m, dst) and topo.chip(m) == topo.chip(c) for m in range(CORES_ALL)))
+        if ok:
+            out.append(c)
+    return out
+
+
+def plan(T, topo):
+    if not _plan:
+        own, cores = T.tables["OWN"], T.cores
+        roads, used = {}, set(cores)
+        for r in range(len(own)):
+            if own[r] == r:
+                continue
+            src, dst = cores[r], cores[own[r]]
+            for p in PIECES:
+                if topo.may_write(src, dst):
+                    roads[(r, p)] = [src, dst]
+                    continue
+                c = [c for c in relays(src, dst, p != "c1", topo) if c not in used][0]
+                used.add(c)
+                roads[(r, p)] = [src, c, dst]
+        _plan["roads"] = roads
+    return _plan["roads"]
+
+
+def rank_program(g, core, T, topo):
+    own, cores = T.tables["OWN"], T.cores
+    roads = plan(T, topo)
+    rank = T.rank_of(core)
+    sem = T.sem
+
+    def engines(src, dst):
+        return topo.mask(src, dst)
+
+    def count(src, dst):
+        return bin(engines(src, dst)).count("1")
+
+    def send(r, piece, hop):
+        road = roads[(r, piece)]
+        src, dst = road[hop], road[hop + 1]
+        a, b = {"c0": (0, W), "c1": (W, 2 * W), "s": (0, 2 * W)}[piece]
+        last = hop + 2 == len(road)
+        if last:
+            k = [p for p in range(len(own)) if own[p] == own[r] and p != own[r]].index(r)
+            base, arr = 2 * W * (k + 1), sem["a%d%s" % (k, piece)]
+        else:
+            base, arr = 0, sem.relay
+        oc, op = (T.mc, T.ms) if last else (T.nc, T.ns)
+        if piece == "s":
+            o, i = op[:, base + a:base + b], T.ns[:, a:b]
+        else:
+            o, i = oc[:, base + a:base + b].bitcast(dt.uint8), T.nc[:, a:b].bitcast(dt.uint8)
+        rid, pid = topo.addr(dst, src)
+        g.remote_dma(o, i, arr, sem.left, pid, rid, engines(src, dst))
+        return count(src, dst)
+
+    if rank is None:
+        for (r, piece), road in roads.items():
+            if len(road) == 3 and road[1] == core:
+                g.wait_ge(sem.relay, count(road[0], core))
+                n = send(r, piece, 1)
+                g.wait_ge(sem.left, n)
+        return
+
+    copy = ActivationFunctionType.Copy
+
+    if own[rank] != rank:
+        for t in range(2):
+            g.sync.dma_start(T.kcb[:, W * t:W * t + W].bitcast(dt.uint8),
+                             T.kc[:, 4 * W * t:4 * W * (t + 1)]).then_inc(sem["lk%d" % t], 16)
+        g.scalar.dma_start(T.ksb[:, 0:2 * W], T.ks[:, 0:2 * W]).then_inc(sem.lks, 16)
+        g.iota(T.idx[:], [[1, W]], 0, -1, allow_small_or_imprecise_dtypes=True).then_inc(sem.iota, 1)
+        g.vector.memset(T.e[:], 0.0).then_inc(sem.zero, 1)
+        g.vector.wait_ge(sem.zero, 1)
+        g.vector.wait_ge(sem.iota, 1)
+        g.vector.tensor_scalar(T.e[:, 3:3 + 4 * W:4], T.idx[:], 0.0, None, AluOpType.is_equal).then_inc(sem.diag, 1)
+        g.vector.wait_ge(sem.diag, 1)
+        for b in range(4):
+            g.vector.quantize_mx(T.sc[:, W * b:W * b + W], T.ss[:, W * b:W * b + W],
+                                 T.e[:, 3 - b:3 - b + 4 * W]).then_inc(sem["sq%d" % b], 1)
+        g.tensor.wait_ge(sem.lks, 16)
+        for t in range(2):
+            g.tensor.wait_ge(sem["lk%d" % t], 16)
+            for b in range(4):
+                if t == 0:
+                    g.tensor.wait_ge(sem["sq%d" % b], 1)
+                i = 4 * t + b
+                g.tensor.matmul_mx(T.ps[:, 512 * i:512 * i + W], T.sc[:, W * b:W * b + W], T.ss[:, W * b:W * b + W],
+                                   T.kcb[:, W * t:W * t + W], T.ksb[:, W * t:W * t + W],
+                                   True, True).then_inc(sem["mm%d" % i], 1)
+        for t in range(2):
+            for b in range(4):
+                i = 4 * t + b
+                o, z = T.kt[:, 4 * W * t + b:4 * W * (t + 1):4], T.ps[:, 512 * i:512 * i + W]
+                if b % 2:
+                    g.vector.wait_ge(sem["mm%d" % i], 1)
+                    g.vector.tensor_scalar(o, z, F, None, AluOpType.mult).then_inc(sem["made%d" % t], 1)
+                else:
+                    g.scalar.wait_ge(sem["mm%d" % i], 1)
+                    g.scalar.activation(o, z, copy, scale=F).then_inc(sem["made%d" % t], 1)
+            g.vector.wait_ge(sem["made%d" % t], 4)
+            g.vector.quantize_mx(T.nc[:, W * t:W * t + W], T.ns[:, W * t:W * t + W],
+                                 T.kt[:, 4 * W * t:4 * W * (t + 1)]).then_inc(sem["packed%d" % t], 1)
+        g.wait_ge(sem.packed0, 1)
+        n = send(rank, "c0", 0)
+        g.wait_ge(sem.packed1, 1)
+        n += send(rank, "c1", 0)
+        n += send(rank, "s", 0)
+        g.wait_ge(sem.iota, 1)
+        g.wait_ge(sem.left, n)
+        return
+
+    g.sync.dma_start(T.qt[:], T.q[:]).then_inc(sem.lq, 16)
+    g.scalar.dma_start(T.ms[:, 0:2 * W], T.ks[:, 0:2 * W]).then_inc(sem.lms, 16)
+    g.sync.dma_start(T.mc[:, 0:2 * W].bitcast(dt.uint8), T.kc[:, 0:8 * W]).then_inc(sem.lmc, 16)
+    g.vector.wait_ge(sem.lq, 16)
+    g.vector.quantize_mx(T.qc[:], T.qs[:], T.qt[:]).then_inc(sem.qq, 1)
+    g.tensor.wait_ge(sem.qq, 1)
+    ps = [p for p in range(len(own)) if own[p] == rank and p != rank]
+    near = sorted(range(3), key=lambda k: (len(roads[(ps[k], "c0")]), not topo.mates(cores[ps[k]], core)))
+    stores = 0
+    for n, k in enumerate([-1] + near):
+        if k < 0:
+            g.tensor.wait_ge(sem.lms, 16)
+            g.tensor.wait_ge(sem.lmc, 16)
+        else:
+            for p in ("c0", "s", "c1"):
+                g.tensor.wait_ge(sem["a%d%s" % (k, p)], count(roads[(ps[k], p)][-2], core))
+        done = sem["cp%d" % n]
+        for t in range(2):
+            a, i = 2 * W * (k + 1) + W * t, 2 * n + t
+            z = T.ps[:, 512 * i:512 * i + W]
+            g.tensor.matmul_mx(z, T.qc[:], T.qs[:], T.mc[:, a:a + W], T.ms[:, a:a + W],
+                               True, True).then_inc(sem["mm%d" % i], 1)
+            if t == 0:
+                g.vector.wait_ge(sem["mm%d" % i], 1)
+                g.vector.tensor_copy(T.yt[:, a:a + W], z).then_inc(done, 1)
+            else:
+                g.scalar.wait_ge(sem["mm%d" % i], 1)
+                g.scalar.activation(T.yt[:, a:a + W], z, copy).then_inc(done, 1)
+        a = 2 * W * (k + 1)
+        g.sync.wait_ge(done, 2)
+        g.sync.dma_start(T.y[:, a:a + 2 * W], T.yt[:, a:a + 2 * W]).then_inc(sem.stored, 16)
+        stores += 16
+    g.sync.wait_ge(sem.stored, stores)

@@ -4,7 +4,7 @@ from concourse.mybir import dt, AluOpType, ActivationFunctionType
 CORES_ALL = 512
 W = 128
 F = float(np.float32(0.7))
-PIECES = ("c0", "c1", "s")
+PIECES = (("c", 0, W, True, False), ("c", W, 2 * W, False, True), ("s", 0, 2 * W, True, True))
 
 SCRATCH = {
     "idx": ("sbuf", [128, 128], "float32"),
@@ -16,6 +16,8 @@ SCRATCH = {
     "kt": ("sbuf", [128, 1024], "bfloat16"),
     "nc": ("sbuf", [128, 256], "float8_e4m3fn_x4"),
     "ns": ("sbuf", [128, 256], "uint8"),
+    "rc": ("sbuf", [128, 256], "float8_e4m3fn_x4"),
+    "rs": ("sbuf", [128, 256], "uint8"),
     "qt": ("sbuf", [128, 512], "bfloat16"),
     "qc": ("sbuf", [128, 128], "float8_e4m3fn_x4"),
     "qs": ("sbuf", [128, 128], "uint8"),
@@ -24,54 +26,57 @@ SCRATCH = {
     "yt": ("sbuf", [128, 1024], "float32"),
     "ps": ("psum", [128, 4096], "float32"),
 }
-SEMAPHORES = (["iota", "zero", "diag", "left", "relay", "lq", "lms", "lmc", "qq", "stored", "lks"]
+SEMAPHORES = (["iota", "zero", "diag", "left", "lq", "lms", "lmc", "qq", "stored", "lks"]
               + ["lk%d" % t for t in range(2)] + ["sq%d" % b for b in range(4)] + ["mm%d" % i for i in range(8)]
-              + ["made%d" % t for t in range(2)] + ["packed%d" % t for t in range(2)]
-              + ["a%d%s" % (k, p) for k in range(3) for p in PIECES] + ["cp%d" % k for k in range(4)])
+              + ["made%d" % t for t in range(2)] + ["packed%d" % t for t in range(2)] + ["relay%d" % j for j in range(4)]
+              + ["a%d_%d" % (k, j) for k in range(3) for j in range(4)] + ["cp%d" % k for k in range(4)])
 
 _plan = {}
 
 
-def relays(src, dst, cable_first, topo):
+def relays(src, dst, cable_first, among, topo):
     out = []
-    for c in range(CORES_ALL):
-        if topo.die(c) == topo.die(src) or not (topo.may_write(src, c) and topo.may_write(c, dst)):
+    for c in among:
+        if not (topo.may_write(src, c) and topo.may_write(c, dst)):
             continue
         across = topo.rack(topo.host(c)) != topo.rack(topo.host(src))
         if topo.host(c) in (topo.host(src), topo.host(dst)) or across != cable_first:
             continue
         if cable_first:
-            ok = topo.chip(c) == topo.chip(src)
+            if topo.chip(c) != topo.chip(src):
+                continue
+            score = 0
         else:
-            ok = topo.same_plane(src, c) and (topo.chip(c) == topo.chip(dst) or any(
-                topo.mates(m, dst) and topo.chip(m) == topo.chip(c) for m in range(CORES_ALL)))
-        if ok:
-            out.append(c)
-    return out
+            score = 0 if topo.chip(c) == topo.chip(dst) else 1 if any(
+                topo.mates(m, dst) and topo.chip(m) == topo.chip(c) for m in range(CORES_ALL)) else 2
+        out.append((score, c))
+    return [c for score, c in sorted(out)]
 
 
 def plan(T, topo):
     if not _plan:
         own, cores = T.tables["OWN"], T.cores
-        roads, used = {}, set(cores)
+        used = {cores[r] for r in range(len(own)) if own[r] == r}
         for r in range(len(own)):
             if own[r] == r:
                 continue
             src, dst = cores[r], cores[own[r]]
-            for p in PIECES:
-                if topo.may_write(src, dst):
-                    roads[(r, p)] = [src, dst]
-                    continue
-                c = [c for c in relays(src, dst, p != "c1", topo) if c not in used][0]
-                used.add(c)
-                roads[(r, p)] = [src, c, dst]
-        _plan["roads"] = roads
-    return _plan["roads"]
+            _plan[r] = []
+            for kind, a, b, first, by_rank in PIECES:
+                road = [src, dst]
+                if not topo.may_write(src, dst):
+                    among = [c for c in range(CORES_ALL) if c not in used and (
+                        c in cores if by_rank else c not in cores and topo.die(c) != topo.die(src))]
+                    c = relays(src, dst, first, among, topo)[0]
+                    used.add(c)
+                    road = [src, c, dst]
+                _plan[r].append((kind, a, b, road))
+    return _plan
 
 
 def rank_program(g, core, T, topo):
     own, cores = T.tables["OWN"], T.cores
-    roads = plan(T, topo)
+    pieces = plan(T, topo)
     rank = T.rank_of(core)
     sem = T.sem
 
@@ -81,31 +86,38 @@ def rank_program(g, core, T, topo):
     def count(src, dst):
         return bin(engines(src, dst)).count("1")
 
-    def send(r, piece, hop):
-        road = roads[(r, piece)]
+    def send(r, j, hop):
+        kind, a, b, road = pieces[r][j]
         src, dst = road[hop], road[hop + 1]
-        a, b = {"c0": (0, W), "c1": (W, 2 * W), "s": (0, 2 * W)}[piece]
         last = hop + 2 == len(road)
         if last:
             k = [p for p in range(len(own)) if own[p] == own[r] and p != own[r]].index(r)
-            base, arr = 2 * W * (k + 1), sem["a%d%s" % (k, piece)]
+            base, arr = 2 * W * (k + 1), sem["a%d_%d" % (k, j)]
         else:
-            base, arr = 0, sem.relay
-        oc, op = (T.mc, T.ms) if last else (T.nc, T.ns)
-        if piece == "s":
-            o, i = op[:, base + a:base + b], T.ns[:, a:b]
+            base, arr = 0, sem["relay%d" % j]
+        oc, op = (T.mc, T.ms) if last else (T.rc, T.rs)
+        ic, ip = (T.rc, T.rs) if hop else (T.nc, T.ns)
+        if kind == "s":
+            o, i = op[:, base + a:base + b], ip[:, a:b]
         else:
-            o, i = oc[:, base + a:base + b].bitcast(dt.uint8), T.nc[:, a:b].bitcast(dt.uint8)
+            o, i = oc[:, base + a:base + b].bitcast(dt.uint8), ic[:, a:b].bitcast(dt.uint8)
         rid, pid = topo.addr(dst, src)
         g.remote_dma(o, i, arr, sem.left, pid, rid, engines(src, dst))
         return count(src, dst)
 
+    def pass_on():
+        n = 0
+        for r in pieces:
+            for j, (kind, a, b, road) in enumerate(pieces[r]):
+                if len(road) == 3 and road[1] == core:
+                    g.wait_ge(sem["relay%d" % j], count(road[0], core))
+                    n += send(r, j, 1)
+        return n
+
     if rank is None:
-        for (r, piece), road in roads.items():
-            if len(road) == 3 and road[1] == core:
-                g.wait_ge(sem.relay, count(road[0], core))
-                n = send(r, piece, 1)
-                g.wait_ge(sem.left, n)
+        n = pass_on()
+        if n:
+            g.wait_ge(sem.left, n)
         return
 
     copy = ActivationFunctionType.Copy
@@ -147,12 +159,14 @@ def rank_program(g, core, T, topo):
             g.vector.wait_ge(sem["made%d" % t], 4)
             g.vector.quantize_mx(T.nc[:, W * t:W * t + W], T.ns[:, W * t:W * t + W],
                                  T.kt[:, 4 * W * t:4 * W * (t + 1)]).then_inc(sem["packed%d" % t], 1)
+        n, ready = 0, 0
         g.wait_ge(sem.packed0, 1)
-        n = send(rank, "c0", 0)
-        g.wait_ge(sem.packed1, 1)
-        n += send(rank, "c1", 0)
-        n += send(rank, "s", 0)
-        g.wait_ge(sem.iota, 1)
+        for j, (kind, a, b, road) in enumerate(pieces[rank]):
+            if b > W and not ready:
+                g.wait_ge(sem.packed1, 1)
+                ready = 1
+            n += send(rank, j, 0)
+        n += pass_on()
         g.wait_ge(sem.left, n)
         return
 
@@ -163,17 +177,18 @@ def rank_program(g, core, T, topo):
     g.vector.quantize_mx(T.qc[:], T.qs[:], T.qt[:]).then_inc(sem.qq, 1)
     g.tensor.wait_ge(sem.qq, 1)
     ps = [p for p in range(len(own)) if own[p] == rank and p != rank]
-    near = sorted(range(3), key=lambda k: (len(roads[(ps[k], "c0")]), not topo.mates(cores[ps[k]], core)))
-    stores = 0
+    near = sorted(range(3), key=lambda k: (len(pieces[ps[k]][0][3]), not topo.mates(cores[ps[k]], core)))
+    stores, seen = 0, set()
     for n, k in enumerate([-1] + near):
         if k < 0:
             g.tensor.wait_ge(sem.lms, 16)
             g.tensor.wait_ge(sem.lmc, 16)
-        else:
-            for p in ("c0", "s", "c1"):
-                g.tensor.wait_ge(sem["a%d%s" % (k, p)], count(roads[(ps[k], p)][-2], core))
         done = sem["cp%d" % n]
         for t in range(2):
+            for j, (kind, a, b, road) in enumerate(pieces[ps[k]] if k >= 0 else ()):
+                if a < W * (t + 1) and b > W * t and (k, j) not in seen:
+                    seen.add((k, j))
+                    g.tensor.wait_ge(sem["a%d_%d" % (k, j)], count(road[-2], core))
             a, i = 2 * W * (k + 1) + W * t, 2 * n + t
             z = T.ps[:, 512 * i:512 * i + W]
             g.tensor.matmul_mx(z, T.qc[:], T.qs[:], T.mc[:, a:a + W], T.ms[:, a:a + W],

@@ -1,13 +1,19 @@
 import numpy as np
+from concourse.bass import DstId, RemoteDMATransfer
 from concourse.mybir import dt, AluOpType, ActivationFunctionType
 
 CORES_ALL = 512
 W = 128
+HALF = W // 2
 F = float(np.float32(0.7))
-PIECES = (("c", 0, W, True, False), ("c", W, 2 * W, False, True), ("s", 0, 2 * W, True, True))
+STRAIGHT = [[("c", 0, W, (0, 1))], [("c", W, 2 * W, (0, 1))], [("s", 0, 2 * W, (0, 1))]]
+AROUND = [[("c", 0, HALF, (0, .5)), ("c", HALF, W, (.5, 1))],
+          [("c", W, W + HALF, (0, .5)), ("c", W + HALF, 2 * W, (.5, 1))],
+          [("s", 0, 2 * W, (0, 1))]]
+ON_RANK, ON_OTHER = (0, 1), (0, .5)
 
 SCRATCH = {
-    "idx": ("sbuf", [128, 128], "float32"),
+    "idx": ("sbuf", [128, 128], "bfloat16"),
     "e": ("sbuf", [128, 516], "bfloat16"),
     "sc": ("sbuf", [128, 512], "float8_e4m3fn_x4"),
     "ss": ("sbuf", [128, 512], "uint8"),
@@ -28,90 +34,101 @@ SCRATCH = {
 }
 SEMAPHORES = (["iota", "zero", "diag", "left", "lq", "lms", "lmc", "qq", "stored", "lks"]
               + ["lk%d" % t for t in range(2)] + ["sq%d" % b for b in range(4)] + ["mm%d" % i for i in range(8)]
-              + ["made%d" % t for t in range(2)] + ["packed%d" % t for t in range(2)] + ["relay%d" % j for j in range(4)]
-              + ["a%d_%d" % (k, j) for k in range(3) for j in range(4)] + ["cp%d" % k for k in range(4)])
+              + ["made%d" % t for t in range(2)] + ["packed%d" % t for t in range(2)] + ["relay%d" % j for j in range(5)]
+              + ["a%d_%d" % (k, j) for k in range(3) for j in range(5)] + ["cp%d" % n for n in range(4)])
 
 _plan = {}
 
 
-def relays(src, dst, cable_first, among, topo):
-    out = []
-    for c in among:
-        if not (topo.may_write(src, c) and topo.may_write(c, dst)):
-            continue
-        across = topo.rack(topo.host(c)) != topo.rack(topo.host(src))
-        if topo.host(c) in (topo.host(src), topo.host(dst)) or across != cable_first:
-            continue
-        if cable_first:
-            if topo.chip(c) != topo.chip(src):
-                continue
-            score = 0
-        else:
-            score = 0 if topo.chip(c) == topo.chip(dst) else 1 if any(
-                topo.mates(m, dst) and topo.chip(m) == topo.chip(c) for m in range(CORES_ALL)) else 2
-        out.append((score, c))
-    return [c for score, c in sorted(out)]
+def between(src, own, cores, topo):
+    def consumer(c):
+        return cores[own[cores.index(c)]]
+    dst = consumer(src)
+    producers = [c for c in cores if consumer(c) != c]
+    diagonal = [c for c in producers if not topo.may_write(c, consumer(c))]
+    ok = [c for c in range(CORES_ALL) if topo.may_write(src, c) and topo.may_write(c, dst)
+          and topo.host(c) not in (topo.host(src), topo.host(dst))]
+    far = [c for c in ok if topo.rack(topo.host(c)) != topo.rack(topo.host(src))]
+    near = [c for c in ok if c not in far]
+    door = [c for c in near if topo.chip(c) == topo.chip(dst)]
+    beside = [c for c in near if any(topo.mates(m, dst) and topo.chip(m) == topo.chip(c) for m in range(CORES_ALL))]
+    by = [c for c in door + beside if c in producers][0]
+    free = [c for c in door if c not in cores][0]
+    cabled = [c for c in far if c in producers and topo.chip(c) == topo.chip(src)][0]
+    place = [c for c in diagonal if topo.host(c) == topo.host(src)].index(src)
+    other = [c for c in diagonal if c in far][place]
+    return [by, free, by, other, cabled]
 
 
 def plan(T, topo):
     if not _plan:
         own, cores = T.tables["OWN"], T.cores
-        used = {cores[r] for r in range(len(own)) if own[r] == r}
         for r in range(len(own)):
             if own[r] == r:
                 continue
             src, dst = cores[r], cores[own[r]]
-            _plan[r] = []
-            for kind, a, b, first, by_rank in PIECES:
-                road = [src, dst]
-                if not topo.may_write(src, dst):
-                    among = [c for c in range(CORES_ALL) if c not in used and (
-                        c in cores if by_rank else c not in cores and topo.die(c) != topo.die(src))]
-                    c = relays(src, dst, first, among, topo)[0]
-                    used.add(c)
-                    road = [src, c, dst]
-                _plan[r].append((kind, a, b, road))
+            direct = topo.may_write(src, dst)
+            via = [] if direct else between(src, own, cores, topo)
+            calls, n = [], 0
+            for call in (STRAIGHT if direct else AROUND):
+                calls.append([])
+                for kind, a, b, share in call:
+                    calls[-1].append((n, kind, a, b, share, [src, dst] if direct else [src, via[n], dst]))
+                    n += 1
+            _plan[r] = calls
     return _plan
 
 
 def rank_program(g, core, T, topo):
     own, cores = T.tables["OWN"], T.cores
-    pieces = plan(T, topo)
+    calls = plan(T, topo)
     rank = T.rank_of(core)
     sem = T.sem
 
-    def engines(src, dst):
-        return topo.mask(src, dst)
+    def engines(piece, hop):
+        src, dst = piece[5][hop], piece[5][hop + 1]
+        share = piece[4] if not hop else ON_RANK if src in cores else ON_OTHER
+        can = [e for e in range(16) if topo.mask(src, dst) >> e & 1]
+        return can[int(share[0] * len(can)):int(share[1] * len(can))]
 
-    def count(src, dst):
-        return bin(engines(src, dst)).count("1")
-
-    def send(r, j, hop):
-        kind, a, b, road = pieces[r][j]
-        src, dst = road[hop], road[hop + 1]
-        last = hop + 2 == len(road)
-        if last:
-            k = [p for p in range(len(own)) if own[p] == own[r] and p != own[r]].index(r)
-            base, arr = 2 * W * (k + 1), sem["a%d_%d" % (k, j)]
+    def send(r, group, hop):
+        out, n = [], 0
+        for piece in group:
+            j, kind, a, b, share, road = piece
+            src, dst = road[hop], road[hop + 1]
+            last = hop + 2 == len(road)
+            if last:
+                k = [p for p in range(len(own)) if own[p] == own[r] and p != own[r]].index(r)
+                base, arr = 2 * W * (k + 1), sem["a%d_%d" % (k, j)]
+            else:
+                base, arr = 0, sem["relay%d" % j]
+            oc, op = (T.mc, T.ms) if last else (T.rc, T.rs)
+            ic, ip = (T.rc, T.rs) if hop else (T.nc, T.ns)
+            if kind == "s":
+                o, i = op[:, base + a:base + b], ip[:, a:b]
+            else:
+                o, i = oc[:, base + a:base + b].bitcast(dt.uint8), ic[:, a:b].bitcast(dt.uint8)
+            used = engines(piece, hop)
+            rid, pid = topo.addr(dst, src)
+            out.append((o, i, arr, pid, rid, sum(1 << e for e in used)))
+            n += len(used)
+        if len(out) == 1:
+            o, i, arr, pid, rid, mask = out[0]
+            g.remote_dma(o, i, arr, sem.left, pid, rid, mask)
         else:
-            base, arr = 0, sem["relay%d" % j]
-        oc, op = (T.mc, T.ms) if last else (T.rc, T.rs)
-        ic, ip = (T.rc, T.rs) if hop else (T.nc, T.ns)
-        if kind == "s":
-            o, i = op[:, base + a:base + b], ip[:, a:b]
-        else:
-            o, i = oc[:, base + a:base + b].bitcast(dt.uint8), ic[:, a:b].bitcast(dt.uint8)
-        rid, pid = topo.addr(dst, src)
-        g.remote_dma(o, i, arr, sem.left, pid, rid, engines(src, dst))
-        return count(src, dst)
+            g.remote_dma_fused([RemoteDMATransfer(dst_ids=[DstId(rid=rid, pnc=pid)], dma_engine_mask=mask, remote_sem=arr,
+                                                  src=i, dst=o) for o, i, arr, pid, rid, mask in out], local_sem=sem.left)
+        return n
 
     def pass_on():
         n = 0
-        for r in pieces:
-            for j, (kind, a, b, road) in enumerate(pieces[r]):
-                if len(road) == 3 and road[1] == core:
-                    g.wait_ge(sem["relay%d" % j], count(road[0], core))
-                    n += send(r, j, 1)
+        for r in calls:
+            for group in calls[r]:
+                for piece in group:
+                    j, road = piece[0], piece[5]
+                    if len(road) == 3 and road[1] == core:
+                        g.wait_ge(sem["relay%d" % j], len(engines(piece, 0)))
+                        n += send(r, [piece], 1)
         return n
 
     if rank is None:
@@ -161,11 +178,11 @@ def rank_program(g, core, T, topo):
                                  T.kt[:, 4 * W * t:4 * W * (t + 1)]).then_inc(sem["packed%d" % t], 1)
         n, ready = 0, 0
         g.wait_ge(sem.packed0, 1)
-        for j, (kind, a, b, road) in enumerate(pieces[rank]):
-            if b > W and not ready:
+        for group in calls[rank]:
+            if not ready and max(piece[3] for piece in group) > W:
                 g.wait_ge(sem.packed1, 1)
                 ready = 1
-            n += send(rank, j, 0)
+            n += send(rank, group, 0)
         n += pass_on()
         g.wait_ge(sem.left, n)
         return
@@ -177,30 +194,30 @@ def rank_program(g, core, T, topo):
     g.vector.quantize_mx(T.qc[:], T.qs[:], T.qt[:]).then_inc(sem.qq, 1)
     g.tensor.wait_ge(sem.qq, 1)
     ps = [p for p in range(len(own)) if own[p] == rank and p != rank]
-    near = sorted(range(3), key=lambda k: (len(pieces[ps[k]][0][3]), not topo.mates(cores[ps[k]], core)))
+    near = sorted(range(3), key=lambda k: (len(calls[ps[k]][0][0][5]), not topo.mates(cores[ps[k]], core)))
     stores, seen = 0, set()
     for n, k in enumerate([-1] + near):
         if k < 0:
             g.tensor.wait_ge(sem.lms, 16)
             g.tensor.wait_ge(sem.lmc, 16)
-        done = sem["cp%d" % n]
         for t in range(2):
-            for j, (kind, a, b, road) in enumerate(pieces[ps[k]] if k >= 0 else ()):
+            for piece in ([p for c in calls[ps[k]] for p in c] if k >= 0 else []):
+                j, kind, a, b, share, road = piece
                 if a < W * (t + 1) and b > W * t and (k, j) not in seen:
                     seen.add((k, j))
-                    g.tensor.wait_ge(sem["a%d_%d" % (k, j)], count(road[-2], core))
+                    g.tensor.wait_ge(sem["a%d_%d" % (k, j)], len(engines(piece, len(road) - 2)))
             a, i = 2 * W * (k + 1) + W * t, 2 * n + t
             z = T.ps[:, 512 * i:512 * i + W]
             g.tensor.matmul_mx(z, T.qc[:], T.qs[:], T.mc[:, a:a + W], T.ms[:, a:a + W],
                                True, True).then_inc(sem["mm%d" % i], 1)
             if t == 0:
                 g.vector.wait_ge(sem["mm%d" % i], 1)
-                g.vector.tensor_copy(T.yt[:, a:a + W], z).then_inc(done, 1)
+                g.vector.tensor_copy(T.yt[:, a:a + W], z).then_inc(sem["cp%d" % n], 1)
             else:
                 g.scalar.wait_ge(sem["mm%d" % i], 1)
-                g.scalar.activation(T.yt[:, a:a + W], z, copy).then_inc(done, 1)
+                g.scalar.activation(T.yt[:, a:a + W], z, copy).then_inc(sem["cp%d" % n], 1)
         a = 2 * W * (k + 1)
-        g.sync.wait_ge(done, 2)
+        g.sync.wait_ge(sem["cp%d" % n], 2)
         g.sync.dma_start(T.y[:, a:a + 2 * W], T.yt[:, a:a + 2 * W]).then_inc(sem.stored, 16)
         stores += 16
     g.sync.wait_ge(sem.stored, stores)

import numpy as np
from concourse.bass import DstId, RemoteDMATransfer
from concourse.mybir import dt, AluOpType, ActivationFunctionType

CORES_ALL = 512
W = 128
HALF = W // 2
F = float(np.float32(0.7))
STRAIGHT = [[("c", 0, W, (0, 1))], [("c", W, 2 * W, (0, 1))], [("s", 0, 2 * W, (0, 1))]]
AROUND = [[("c", 0, HALF, (0, .5)), ("c", HALF, W, (.5, 1))],
          [("c", W, W + HALF, (0, .5)), ("c", W + HALF, 2 * W, (.5, 1))],
          [("s", 0, 2 * W, (0, 1))]]
ON_RANK, ON_OTHER = (0, 1), (0, .5)

SCRATCH = {
    "idx": ("sbuf", [128, 128], "bfloat16"),
    "e": ("sbuf", [128, 516], "bfloat16"),
    "sc": ("sbuf", [128, 512], "float8_e4m3fn_x4"),
    "ss": ("sbuf", [128, 512], "uint8"),
    "kcb": ("sbuf", [128, 256], "float8_e4m3fn_x4"),
    "ksb": ("sbuf", [128, 256], "uint8"),
    "kt": ("sbuf", [128, 1024], "bfloat16"),
    "nc": ("sbuf", [128, 256], "float8_e4m3fn_x4"),
    "ns": ("sbuf", [128, 256], "uint8"),
    "rc": ("sbuf", [128, 256], "float8_e4m3fn_x4"),
    "rs": ("sbuf", [128, 256], "uint8"),
    "qt": ("sbuf", [128, 512], "bfloat16"),
    "qc": ("sbuf", [128, 128], "float8_e4m3fn_x4"),
    "qs": ("sbuf", [128, 128], "uint8"),
    "mc": ("sbuf", [128, 1024], "float8_e4m3fn_x4"),
    "ms": ("sbuf", [128, 1024], "uint8"),
    "yt": ("sbuf", [128, 1024], "float32"),
    "ps": ("psum", [128, 4096], "float32"),
}
SEMAPHORES = (["iota", "zero", "diag", "left", "lq", "lms", "lmc", "qq", "stored", "lks"]
              + ["lk%d" % t for t in range(2)] + ["sq%d" % b for b in range(4)] + ["mm%d" % i for i in range(8)]
              + ["made%d" % t for t in range(2)] + ["packed%d" % t for t in range(2)] + ["relay%d" % j for j in range(5)]
              + ["a%d_%d" % (k, j) for k in range(3) for j in range(5)] + ["cp%d" % n for n in range(4)])

_plan = {}


def between(src, own, cores, topo):
    def consumer(c):
        return cores[own[cores.index(c)]]
    dst = consumer(src)
    producers = [c for c in cores if consumer(c) != c]
    diagonal = [c for c in producers if not topo.may_write(c, consumer(c))]
    ok = [c for c in range(CORES_ALL) if topo.may_write(src, c) and topo.may_write(c, dst)
          and topo.host(c) not in (topo.host(src), topo.host(dst))]
    far = [c for c in ok if topo.rack(topo.host(c)) != topo.rack(topo.host(src))]
    near = [c for c in ok if c not in far]
    door = [c for c in near if topo.chip(c) == topo.chip(dst)]
    beside = [c for c in near if any(topo.mates(m, dst) and topo.chip(m) == topo.chip(c) for m in range(CORES_ALL))]
    by = [c for c in door + beside if c in producers][0]
    free = [c for c in door if c not in cores][0]
    cabled = [c for c in far if c in producers and topo.chip(c) == topo.chip(src)][0]
    place = [c for c in diagonal if topo.host(c) == topo.host(src)].index(src)
    other = [c for c in diagonal if c in far][place]
    return [by, free, by, other, cabled]


def plan(T, topo):
    if not _plan:
        own, cores = T.tables["OWN"], T.cores
        for r in range(len(own)):
            if own[r] == r:
                continue
            src, dst = cores[r], cores[own[r]]
            direct = topo.may_write(src, dst)
            via = [] if direct else between(src, own, cores, topo)
            calls, n = [], 0
            for call in (STRAIGHT if direct else AROUND):
                calls.append([])
                for kind, a, b, share in call:
                    calls[-1].append((n, kind, a, b, share, [src, dst] if direct else [src, via[n], dst]))
                    n += 1
            _plan[r] = calls
    return _plan


def rank_program(g, core, T, topo):
    own, cores = T.tables["OWN"], T.cores
    calls = plan(T, topo)
    rank = T.rank_of(core)
    sem = T.sem

    def engines(piece, hop):
        src, dst = piece[5][hop], piece[5][hop + 1]
        share = piece[4] if not hop else ON_RANK if src in cores else ON_OTHER
        can = [e for e in range(16) if topo.mask(src, dst) >> e & 1]
        return can[int(share[0] * len(can)):int(share[1] * len(can))]

    def send(r, group, hop):
        out, n = [], 0
        for piece in group:
            j, kind, a, b, share, road = piece
            src, dst = road[hop], road[hop + 1]
            last = hop + 2 == len(road)
            if last:
                k = [p for p in range(len(own)) if own[p] == own[r] and p != own[r]].index(r)
                base, arr = 2 * W * (k + 1), sem["a%d_%d" % (k, j)]
            else:
                base, arr = 0, sem["relay%d" % j]
            oc, op = (T.mc, T.ms) if last else (T.rc, T.rs)
            ic, ip = (T.rc, T.rs) if hop else (T.nc, T.ns)
            if kind == "s":
                o, i = op[:, base + a:base + b], ip[:, a:b]
            else:
                o, i = oc[:, base + a:base + b].bitcast(dt.uint8), ic[:, a:b].bitcast(dt.uint8)
            used = engines(piece, hop)
            rid, pid = topo.addr(dst, src)
            out.append((o, i, arr, pid, rid, sum(1 << e for e in used)))
            n += len(used)
        if len(out) == 1:
            o, i, arr, pid, rid, mask = out[0]
            g.remote_dma(o, i, arr, sem.left, pid, rid, mask)
        else:
            g.remote_dma_fused([RemoteDMATransfer(dst_ids=[DstId(rid=rid, pnc=pid)], dma_engine_mask=mask, remote_sem=arr,
                                                  src=i, dst=o) for o, i, arr, pid, rid, mask in out], local_sem=sem.left)
        return n

    def pass_on():
        n = 0
        for r in calls:
            for group in calls[r]:
                for piece in group:
                    j, road = piece[0], piece[5]
                    if len(road) == 3 and road[1] == core:
                        g.wait_ge(sem["relay%d" % j], len(engines(piece, 0)))
                        n += send(r, [piece], 1)
        return n

    if rank is None:
        n = pass_on()
        if n:
            g.wait_ge(sem.left, n)
        return

    copy = ActivationFunctionType.Copy

    if own[rank] != rank:
        for t in range(2):
            g.sync.dma_start(T.kcb[:, W * t:W * t + W].bitcast(dt.uint8),
                             T.kc[:, 4 * W * t:4 * W * (t + 1)]).then_inc(sem["lk%d" % t], 16)
        g.scalar.dma_start(T.ksb[:, 0:2 * W], T.ks[:, 0:2 * W]).then_inc(sem.lks, 16)
        g.iota(T.idx[:], [[1, W]], 0, -1, allow_small_or_imprecise_dtypes=True).then_inc(sem.iota, 1)
        g.vector.memset(T.e[:], 0.0).then_inc(sem.zero, 1)
        g.vector.wait_ge(sem.zero, 1)
        g.vector.wait_ge(sem.iota, 1)
        g.vector.tensor_scalar(T.e[:, 3:3 + 4 * W:4], T.idx[:], 0.0, None, AluOpType.is_equal).then_inc(sem.diag, 1)
        g.vector.wait_ge(sem.diag, 1)
        for b in range(4):
            g.vector.quantize_mx(T.sc[:, W * b:W * b + W], T.ss[:, W * b:W * b + W],
                                 T.e[:, 3 - b:3 - b + 4 * W]).then_inc(sem["sq%d" % b], 1)
        g.tensor.wait_ge(sem.lks, 16)
        for t in range(2):
            g.tensor.wait_ge(sem["lk%d" % t], 16)
            for b in range(4):
                if t == 0:
                    g.tensor.wait_ge(sem["sq%d" % b], 1)
                i = 4 * t + b
                g.tensor.matmul_mx(T.ps[:, 512 * i:512 * i + W], T.sc[:, W * b:W * b + W], T.ss[:, W * b:W * b + W],
                                   T.kcb[:, W * t:W * t + W], T.ksb[:, W * t:W * t + W],
                                   True, True).then_inc(sem["mm%d" % i], 1)
        for t in range(2):
            for b in range(4):
                i = 4 * t + b
                o, z = T.kt[:, 4 * W * t + b:4 * W * (t + 1):4], T.ps[:, 512 * i:512 * i + W]
                if b % 2:
                    g.vector.wait_ge(sem["mm%d" % i], 1)
                    g.vector.tensor_scalar(o, z, F, None, AluOpType.mult).then_inc(sem["made%d" % t], 1)
                else:
                    g.scalar.wait_ge(sem["mm%d" % i], 1)
                    g.scalar.activation(o, z, copy, scale=F).then_inc(sem["made%d" % t], 1)
            g.vector.wait_ge(sem["made%d" % t], 4)
            g.vector.quantize_mx(T.nc[:, W * t:W * t + W], T.ns[:, W * t:W * t + W],
                                 T.kt[:, 4 * W * t:4 * W * (t + 1)]).then_inc(sem["packed%d" % t], 1)
        n, ready = 0, 0
        g.wait_ge(sem.packed0, 1)
        for group in calls[rank]:
            if not ready and max(piece[3] for piece in group) > W:
                g.wait_ge(sem.packed1, 1)
                ready = 1
            n += send(rank, group, 0)
        n += pass_on()
        g.wait_ge(sem.left, n)
        return

    g.sync.dma_start(T.qt[:], T.q[:]).then_inc(sem.lq, 16)
    g.scalar.dma_start(T.ms[:, 0:2 * W], T.ks[:, 0:2 * W]).then_inc(sem.lms, 16)
    g.sync.dma_start(T.mc[:, 0:2 * W].bitcast(dt.uint8), T.kc[:, 0:8 * W]).then_inc(sem.lmc, 16)
    g.vector.wait_ge(sem.lq, 16)
    g.vector.quantize_mx(T.qc[:], T.qs[:], T.qt[:]).then_inc(sem.qq, 1)
    g.tensor.wait_ge(sem.qq, 1)
    ps = [p for p in range(len(own)) if own[p] == rank and p != rank]
    near = sorted(range(3), key=lambda k: (len(calls[ps[k]][0][0][5]), not topo.mates(cores[ps[k]], core)))
    stores, seen = 0, set()
    for n, k in enumerate([-1] + near):
        if k < 0:
            g.tensor.wait_ge(sem.lms, 16)
            g.tensor.wait_ge(sem.lmc, 16)
        for t in range(2):
            for piece in ([p for c in calls[ps[k]] for p in c] if k >= 0 else []):
                j, kind, a, b, share, road = piece
                if a < W * (t + 1) and b > W * t and (k, j) not in seen:
                    seen.add((k, j))
                    g.tensor.wait_ge(sem["a%d_%d" % (k, j)], len(engines(piece, len(road) - 2)))
            a, i = 2 * W * (k + 1) + W * t, 2 * n + t
            z = T.ps[:, 512 * i:512 * i + W]
            g.tensor.matmul_mx(z, T.qc[:], T.qs[:], T.mc[:, a:a + W], T.ms[:, a:a + W],
                               True, True).then_inc(sem["mm%d" % i], 1)
            if t == 0:
                g.vector.wait_ge(sem["mm%d" % i], 1)
                g.vector.tensor_copy(T.yt[:, a:a + W], z).then_inc(sem["cp%d" % n], 1)
            else:
                g.scalar.wait_ge(sem["mm%d" % i], 1)
                g.scalar.activation(T.yt[:, a:a + W], z, copy).then_inc(sem["cp%d" % n], 1)
        a = 2 * W * (k + 1)
        g.sync.wait_ge(sem["cp%d" % n], 2)
        g.sync.dma_start(T.y[:, a:a + 2 * W], T.yt[:, a:a + 2 * W]).then_inc(sem.stored, 16)
        stores += 16
    g.sync.wait_ge(sem.stored, stores)
